import numpy as np
import ml_dtypes

BF16 = ml_dtypes.bfloat16


def bf(x):
    return np.asarray(x, np.float32).astype(BF16)


def f32(x):
    return np.asarray(x, np.float32)


def f64(x):
    return np.asarray(x).astype(np.float64)


def striped(idx):
    return np.tile(idx.reshape(-1, 16).T, (8, 1))


def rows(idx, k):
    return np.tile(idx, (k, 1))


def look(tab, idx):
    return np.take_along_axis(f64(tab), rows(idx, len(tab)), axis=1)


K, S, V, N, M = 256, 2048, 1536, 1536, 512


def setup_inputs():
    return {"tab": f32(np.random.standard_normal((K, S))), "w": bf(np.random.standard_normal((K, M)) / np.sqrt(K)), "b": f32(0.5 * np.random.standard_normal((M, 1))), "offs": striped(np.random.randint(0, S, N))}


def reference(tab, w, b, offs):
    idx = offs[:16].T.reshape(-1)
    t = look(tab, idx)
    x = np.minimum(np.maximum(t, -1.25), 1.0)
    y = f64(w).T @ x
    return y + f64(b)

@@ -1,0 +1,62 @@
+import concourse.mybir as mybir
+
+F32, BF16, U16 = mybir.dt.float32, mybir.dt.bfloat16, mybir.dt.uint16
+ALU = mybir.AluOpType
+ACT = mybir.ActivationFunctionType
+
+P = 128
+K, S, N, M = 256, 2048, 1536, 512
+BLOCKS = K // P
+CHUNKS = M // P
+PIECE = 512
+LOW, HIGH = -1.25, 1.0
+FLOPS = 2 * K * M * N
+
+
+def tile_lookup_deq_clip_bias_kernel(tc, tab, w, b, offs, out):
+    nc = tc.nc
+    tab_blocks = tab.rearrange("(p k) s -> k p s", k=BLOCKS)
+    w_blocks = w.rearrange("(p k) m -> k p m", k=BLOCKS)
+    out_chunks = out.rearrange("(p c) n -> c p n", c=CHUNKS)
+    with (
+        tc.tile_pool(name="held", bufs=1) as held,
+        tc.tile_pool(name="work", bufs=N // PIECE) as work,
+        tc.psum_pool(name="psum", bufs=2) as psum,
+    ):
+        offsets = held.tile([P, N // 16], U16, name="offsets")
+        nc.sync.dma_start(offsets[:], offs)
+        windows, weights = [], []
+        for k in range(BLOCKS):
+            window = held.tile([P, S], F32, name=f"window{k}")
+            nc.sync.dma_start(window[:], tab_blocks[k])
+            weight = held.tile([P, M], BF16, name=f"weight{k}")
+            nc.sync.dma_start(weight[:], w_blocks[k])
+            windows.append(window)
+            weights.append(weight)
+        bias = held.tile([P, CHUNKS], F32, name="bias")
+        nc.sync.dma_start(bias[:], b.rearrange("(p c) one -> p (c one)", c=CHUNKS))
+
+        for first in range(0, N, PIECE):
+            piece_offsets = offsets[:, first // 16 : (first + PIECE) // 16]
+            banks = [psum.tile([P, PIECE], F32, name=f"bank{c}") for c in range(CHUNKS)]
+            for k in range(BLOCKS):
+                clamped = work.tile([P, PIECE], F32, name=f"clamped{k}")
+                nc.vector.tensor_scalar(
+                    clamped[:], windows[k][:].indirect(piece_offsets), LOW, HIGH, ALU.max, ALU.min
+                )
+                rounded = work.tile([P, PIECE], BF16, name=f"rounded{k}")
+                if k == 0:
+                    nc.scalar.copy(rounded[:], clamped[:])
+                else:
+                    nc.vector.tensor_copy(rounded[:], clamped[:])
+                for c in range(CHUNKS):
+                    nc.tensor.matmul(
+                        banks[c][:], weights[k][:, c::CHUNKS], rounded[:], start=k == 0, stop=k == BLOCKS - 1
+                    )
+            for c in range(CHUNKS):
+                result = work.tile([P, PIECE], F32, name=f"result{c}")
+                if c < CHUNKS - 1:
+                    nc.scalar.activation(result[:], banks[c][:], ACT.Identity, bias=bias[:, c : c + 1])
+                else:
+                    nc.vector.tensor_scalar_add(result[:], banks[c][:], bias[:, c : c + 1])
+                nc.sync.dma_start(out_chunks[c][:, first : first + PIECE], result[:])

@@ -8,7 +8,12 @@ P = 128
 K, S, N, M = 256, 2048, 1536, 512
 BLOCKS = K // P
 CHUNKS = M // P
-PIECE = 512
+BANK = 512
+PSUM_BANKS = 8
+EARLY = (128, 128, 256, 512)
+LATE = (256, 256)
+STEP = 256
+RING = 3
 LOW, HIGH = -1.25, 1.0
 FLOPS = 2 * K * M * N
 
@@ -17,46 +22,68 @@ def tile_lookup_deq_clip_bias_kernel(tc, tab, w, b, offs, out):
     nc = tc.nc
     tab_blocks = tab.rearrange("(p k) s -> k p s", k=BLOCKS)
     w_blocks = w.rearrange("(p k) m -> k p m", k=BLOCKS)
-    out_chunks = out.rearrange("(p c) n -> c p n", c=CHUNKS)
+    out_rows = out.rearrange("(p c) n -> p c n", c=CHUNKS)
     with (
         tc.tile_pool(name="held", bufs=1) as held,
-        tc.tile_pool(name="work", bufs=N // PIECE) as work,
-        tc.psum_pool(name="psum", bufs=2) as psum,
+        tc.psum_pool(name="psum", bufs=PSUM_BANKS) as psum,
     ):
         offsets = held.tile([P, N // 16], U16, name="offsets")
-        nc.sync.dma_start(offsets[:], offs)
-        windows, weights = [], []
-        for k in range(BLOCKS):
-            window = held.tile([P, S], F32, name=f"window{k}")
-            nc.sync.dma_start(window[:], tab_blocks[k])
-            weight = held.tile([P, M], BF16, name=f"weight{k}")
-            nc.sync.dma_start(weight[:], w_blocks[k])
-            windows.append(window)
-            weights.append(weight)
+        windows = [held.tile([P, S], F32, name=f"window{k}") for k in range(BLOCKS)]
+        weights = [held.tile([P, M], BF16, name=f"weight{k}") for k in range(BLOCKS)]
         bias = held.tile([P, CHUNKS], F32, name="bias")
-        nc.sync.dma_start(bias[:], b.rearrange("(p c) one -> p (c one)", c=CHUNKS))
+        nc.sync.dma_start(offsets[:], offs)
+        nc.scalar.dma_start(bias[:], b.rearrange("(p c) one -> p (c one)", c=CHUNKS))
+        nc.sync.dma_start(weights[0][:], w_blocks[0])
+        for k in range(BLOCKS):
+            nc.sync.dma_start(windows[k][:], tab_blocks[k])
+        nc.sync.dma_start(weights[1][:], w_blocks[1])
 
-        for first in range(0, N, PIECE):
-            piece_offsets = offsets[:, first // 16 : (first + PIECE) // 16]
-            banks = [psum.tile([P, PIECE], F32, name=f"bank{c}") for c in range(CHUNKS)]
-            for k in range(BLOCKS):
-                clamped = work.tile([P, PIECE], F32, name=f"clamped{k}")
-                nc.vector.tensor_scalar(
-                    clamped[:], windows[k][:].indirect(piece_offsets), LOW, HIGH, ALU.max, ALU.min
-                )
-                rounded = work.tile([P, PIECE], BF16, name=f"rounded{k}")
-                if k == 0:
-                    nc.scalar.copy(rounded[:], clamped[:])
+        widths = EARLY + LATE
+        pieces = [(sum(widths[:i]), width) for i, width in enumerate(widths)]
+        early, late = pieces[: len(EARLY)], pieces[len(EARLY) :]
+        order = [(k, piece) for k in range(BLOCKS) for piece in early]
+        order += [(k, piece) for piece in late for k in range(BLOCKS)]
+
+        ring = [held.tile([P, STEP], F32, name=f"clamped{i}") for i in range(RING)]
+        turn = 0
+        banks_of = {}
+        for k, (first, width) in order:
+            per_bank = BANK // width
+            if k == 0:
+                banks_of[first] = [
+                    psum.tile([P, per_bank, width], F32, name="bank") for j in range(CHUNKS // per_bank)
+                ]
+            banks = banks_of[first]
+            rounded = held.tile([P, width], BF16, name=f"rounded{k}_{first}")
+            step = min(width, STEP)
+            for lo in range(0, width, step):
+                cols = slice(lo, lo + step)
+                clamped = ring[turn % RING][:, :step]
+                turn += 1
+                step_offsets = offsets[:, (first + lo) // 16 : (first + lo + step) // 16]
+                nc.vector.tensor_scalar(clamped, windows[k][:].indirect(step_offsets), LOW, HIGH, ALU.max, ALU.min)
+                if (k == 0 and (first, width) in early) or width < STEP:
+                    nc.scalar.copy(rounded[:, cols], clamped)
                 else:
-                    nc.vector.tensor_copy(rounded[:], clamped[:])
+                    nc.vector.tensor_copy(rounded[:, cols], clamped)
                 for c in range(CHUNKS):
                     nc.tensor.matmul(
-                        banks[c][:], weights[k][:, c::CHUNKS], rounded[:], start=k == 0, stop=k == BLOCKS - 1
+                        banks[c // per_bank][:, c % per_bank, cols],
+                        weights[k][:, c::CHUNKS],
+                        rounded[:, cols],
+                        start=k == 0 and lo == 0 and c % per_bank == 0,
+                        stop=k == BLOCKS - 1 and lo + step == width and c % per_bank == per_bank - 1,
                     )
-            for c in range(CHUNKS):
-                result = work.tile([P, PIECE], F32, name=f"result{c}")
-                if c < CHUNKS - 1:
-                    nc.scalar.activation(result[:], banks[c][:], ACT.Identity, bias=bias[:, c : c + 1])
-                else:
-                    nc.vector.tensor_scalar_add(result[:], banks[c][:], bias[:, c : c + 1])
-                nc.sync.dma_start(out_chunks[c][:, first : first + PIECE], result[:])
+            if k < BLOCKS - 1:
+                continue
+            for j, bank in enumerate(banks):
+                result = held.tile([P, per_bank, width], F32, name=f"result{first}_{j}")
+                for slot in range(per_bank):
+                    c = j * per_bank + slot
+                    if first + width == N and j == len(banks) - 1:
+                        nc.vector.tensor_scalar_add(result[:, slot, :], bank[:, slot, :], bias[:, c : c + 1])
+                    else:
+                        nc.scalar.activation(
+                            result[:, slot, :], bank[:, slot, :], ACT.Identity, bias=bias[:, c : c + 1]
+                        )
+                nc.sync.dma_start(out_rows[:, j * per_bank : (j + 1) * per_bank, first : first + width], result[:])

@@ -9,9 +9,9 @@ K, S, N, M = 256, 2048, 1536, 512
 BLOCKS = K // P
 CHUNKS = M // P
 BANK = 512
-PSUM_BANKS = 8
-EARLY = (128, 128, 256, 512)
-LATE = (256, 256)
+PSUM_BANKS = 6
+EARLY = (128, 384, 512)
+LATE = (512,)
 STEP = 256
 RING = 3
 LOW, HIGH = -1.25, 1.0
@@ -33,10 +33,9 @@ def tile_lookup_deq_clip_bias_kernel(tc, tab, w, b, offs, out):
         bias = held.tile([P, CHUNKS], F32, name="bias")
         nc.sync.dma_start(offsets[:], offs)
         nc.scalar.dma_start(bias[:], b.rearrange("(p c) one -> p (c one)", c=CHUNKS))
-        nc.sync.dma_start(weights[0][:], w_blocks[0])
         for k in range(BLOCKS):
             nc.sync.dma_start(windows[k][:], tab_blocks[k])
-        nc.sync.dma_start(weights[1][:], w_blocks[1])
+            nc.sync.dma_start(weights[k][:], w_blocks[k])
 
         widths = EARLY + LATE
         pieces = [(sum(widths[:i]), width) for i, width in enumerate(widths)]
@@ -55,14 +54,14 @@ def tile_lookup_deq_clip_bias_kernel(tc, tab, w, b, offs, out):
                 ]
             banks = banks_of[first]
             rounded = held.tile([P, width], BF16, name=f"rounded{k}_{first}")
-            step = min(width, STEP)
+            step = width if width <= STEP else width // 2
             for lo in range(0, width, step):
                 cols = slice(lo, lo + step)
                 clamped = ring[turn % RING][:, :step]
                 turn += 1
                 step_offsets = offsets[:, (first + lo) // 16 : (first + lo + step) // 16]
                 nc.vector.tensor_scalar(clamped, windows[k][:].indirect(step_offsets), LOW, HIGH, ALU.max, ALU.min)
-                if (k == 0 and (first, width) in early) or width < STEP:
+                if (k == 0 and (first, width) in early) or first == 0:
                     nc.scalar.copy(rounded[:, cols], clamped)
                 else:
                     nc.vector.tensor_copy(rounded[:, cols], clamped)
@@ -80,7 +79,7 @@ def tile_lookup_deq_clip_bias_kernel(tc, tab, w, b, offs, out):
                 result = held.tile([P, per_bank, width], F32, name=f"result{first}_{j}")
                 for slot in range(per_bank):
                     c = j * per_bank + slot
-                    if first + width == N and j == len(banks) - 1:
+                    if first + width == N and j % 2 == 1:
                         nc.vector.tensor_scalar_add(result[:, slot, :], bank[:, slot, :], bias[:, c : c + 1])
                     else:
                         nc.scalar.activation(

@@ -13,7 +13,7 @@ PSUM_BANKS = 6
 EARLY = (128, 384, 512)
 LATE = (512,)
 STEP = 256
-RING = 3
+RING = 5
 LOW, HIGH = -1.25, 1.0
 FLOPS = 2 * K * M * N
 
@@ -64,7 +64,7 @@ def tile_lookup_deq_clip_bias_kernel(tc, tab, w, b, offs, out):
                 if (k == 0 and (first, width) in early) or first == 0:
                     nc.scalar.copy(rounded[:, cols], clamped)
                 else:
-                    nc.vector.tensor_copy(rounded[:, cols], clamped)
+                    nc.gpsimd.tensor_scalar(rounded[:, cols], clamped, 1.0, 0.0, ALU.mult, ALU.add)
                 for c in range(CHUNKS):
                     nc.tensor.matmul(
                         banks[c // per_bank][:, c % per_bank, cols],

@@ -22,7 +22,7 @@ def tile_lookup_deq_clip_bias_kernel(tc, tab, w, b, offs, out):
     nc = tc.nc
     tab_blocks = tab.rearrange("(p k) s -> k p s", k=BLOCKS)
     w_blocks = w.rearrange("(p k) m -> k p m", k=BLOCKS)
-    out_rows = out.rearrange("(p c) n -> p c n", c=CHUNKS)
+    out_chunks = out.rearrange("(p c) n -> c p n", c=CHUNKS)
     with (
         tc.tile_pool(name="held", bufs=1) as held,
         tc.psum_pool(name="psum", bufs=PSUM_BANKS) as psum,
@@ -32,10 +32,10 @@ def tile_lookup_deq_clip_bias_kernel(tc, tab, w, b, offs, out):
         weights = [held.tile([P, M], BF16, name=f"weight{k}") for k in range(BLOCKS)]
         bias = held.tile([P, CHUNKS], F32, name="bias")
         nc.sync.dma_start(offsets[:], offs)
-        nc.scalar.dma_start(bias[:], b.rearrange("(p c) one -> p (c one)", c=CHUNKS))
         for k in range(BLOCKS):
             nc.sync.dma_start(windows[k][:], tab_blocks[k])
             nc.sync.dma_start(weights[k][:], w_blocks[k])
+        nc.sync.dma_start(bias[:], b.rearrange("(p c) one -> p (c one)", c=CHUNKS))
 
         widths = EARLY + LATE
         pieces = [(sum(widths[:i]), width) for i, width in enumerate(widths)]
@@ -75,14 +75,11 @@ def tile_lookup_deq_clip_bias_kernel(tc, tab, w, b, offs, out):
                     )
             if k < BLOCKS - 1:
                 continue
-            for j, bank in enumerate(banks):
-                result = held.tile([P, per_bank, width], F32, name=f"result{first}_{j}")
-                for slot in range(per_bank):
-                    c = j * per_bank + slot
-                    if first + width == N and j % 2 == 1:
-                        nc.vector.tensor_scalar_add(result[:, slot, :], bank[:, slot, :], bias[:, c : c + 1])
-                    else:
-                        nc.scalar.activation(
-                            result[:, slot, :], bank[:, slot, :], ACT.Identity, bias=bias[:, c : c + 1]
-                        )
-                nc.sync.dma_start(out_rows[:, j * per_bank : (j + 1) * per_bank, first : first + width], result[:])
+            for c in range(CHUNKS):
+                product = banks[c // per_bank][:, c % per_bank, :]
+                result = held.tile([P, width], F32, name=f"result{first}_{c}")
+                if first + width == N and c % 2 == 1:
+                    nc.vector.tensor_scalar_add(result[:], product, bias[:, c : c + 1])
+                else:
+                    nc.scalar.activation(result[:], product, ACT.Identity, bias=bias[:, c : c + 1])
+                nc.sync.dma_start(out_chunks[c][:, first : first + width], result[:])

import concourse.mybir as mybir

F32, BF16, U16 = mybir.dt.float32, mybir.dt.bfloat16, mybir.dt.uint16
ALU = mybir.AluOpType
ACT = mybir.ActivationFunctionType

P = 128
K, S, N, M = 256, 2048, 1536, 512
BLOCKS = K // P
CHUNKS = M // P
BANK = 512
PSUM_BANKS = 6
EARLY = (128, 384, 512)
LATE = (512,)
STEP = 256
RING = 5
LOW, HIGH = -1.25, 1.0
FLOPS = 2 * K * M * N


def tile_lookup_deq_clip_bias_kernel(tc, tab, w, b, offs, out):
    nc = tc.nc
    tab_blocks = tab.rearrange("(p k) s -> k p s", k=BLOCKS)
    w_blocks = w.rearrange("(p k) m -> k p m", k=BLOCKS)
    out_chunks = out.rearrange("(p c) n -> c p n", c=CHUNKS)
    with (
        tc.tile_pool(name="held", bufs=1) as held,
        tc.psum_pool(name="psum", bufs=PSUM_BANKS) as psum,
    ):
        offsets = held.tile([P, N // 16], U16, name="offsets")
        windows = [held.tile([P, S], F32, name=f"window{k}") for k in range(BLOCKS)]
        weights = [held.tile([P, M], BF16, name=f"weight{k}") for k in range(BLOCKS)]
        bias = held.tile([P, CHUNKS], F32, name="bias")
        nc.sync.dma_start(offsets[:], offs)
        for k in range(BLOCKS):
            nc.sync.dma_start(windows[k][:], tab_blocks[k])
            nc.sync.dma_start(weights[k][:], w_blocks[k])
        nc.sync.dma_start(bias[:], b.rearrange("(p c) one -> p (c one)", c=CHUNKS))

        widths = EARLY + LATE
        pieces = [(sum(widths[:i]), width) for i, width in enumerate(widths)]
        early, late = pieces[: len(EARLY)], pieces[len(EARLY) :]
        order = [(k, piece) for k in range(BLOCKS) for piece in early]
        order += [(k, piece) for piece in late for k in range(BLOCKS)]

        ring = [held.tile([P, STEP], F32, name=f"clamped{i}") for i in range(RING)]
        turn = 0
        banks_of = {}
        for k, (first, width) in order:
            per_bank = BANK // width
            if k == 0:
                banks_of[first] = [
                    psum.tile([P, per_bank, width], F32, name="bank") for j in range(CHUNKS // per_bank)
                ]
            banks = banks_of[first]
            rounded = held.tile([P, width], BF16, name=f"rounded{k}_{first}")
            step = width if width <= STEP else width // 2
            for lo in range(0, width, step):
                cols = slice(lo, lo + step)
                clamped = ring[turn % RING][:, :step]
                turn += 1
                step_offsets = offsets[:, (first + lo) // 16 : (first + lo + step) // 16]
                nc.vector.tensor_scalar(clamped, windows[k][:].indirect(step_offsets), LOW, HIGH, ALU.max, ALU.min)
                if (k == 0 and (first, width) in early) or first == 0:
                    nc.scalar.copy(rounded[:, cols], clamped)
                else:
                    nc.gpsimd.tensor_scalar(rounded[:, cols], clamped, 1.0, 0.0, ALU.mult, ALU.add)
                for c in range(CHUNKS):
                    nc.tensor.matmul(
                        banks[c // per_bank][:, c % per_bank, cols],
                        weights[k][:, c::CHUNKS],
                        rounded[:, cols],
                        start=k == 0 and lo == 0 and c % per_bank == 0,
                        stop=k == BLOCKS - 1 and lo + step == width and c % per_bank == per_bank - 1,
                    )
            if k < BLOCKS - 1:
                continue
            for c in range(CHUNKS):
                product = banks[c // per_bank][:, c % per_bank, :]
                result = held.tile([P, width], F32, name=f"result{first}_{c}")
                if first + width == N and c % 2 == 1:
                    nc.vector.tensor_scalar_add(result[:], product, bias[:, c : c + 1])
                else:
                    nc.scalar.activation(result[:], product, ACT.Identity, bias=bias[:, c : c + 1])
                nc.sync.dma_start(out_chunks[c][:, first : first + width], result[:])
